import numpy as np
import ml_dtypes


def mxq(x, axis, fmt="e4m3"):
    dtype, down = {"e4m3": (ml_dtypes.float8_e4m3fn, 7), "e5m2": (ml_dtypes.float8_e5m2, 14)}[fmt]
    v = np.moveaxis(np.asarray(x, np.float32).astype(ml_dtypes.bfloat16).astype(np.float64), axis, -1)
    blocks = v.reshape(v.shape[:-1] + (-1, 32))
    amax = np.abs(blocks).max(-1, keepdims=True)
    byte = np.maximum(np.where(amax > 0, np.frexp(amax)[1] - 1 + 127, 0) - down, 1)
    scale = np.exp2(byte - 127.0)
    codes = (blocks / scale).astype(np.float32).astype(dtype).astype(np.float64)
    return np.moveaxis((codes * scale).reshape(v.shape), -1, axis)


WIDE = False


def mx_kscale(k):
    if not WIDE:
        return np.ones(k)
    levels = np.array([10, -10, 5, -5, 0])
    if k % 512:
        return np.exp2(np.random.permutation(np.resize(levels, k // 32))).repeat(32)
    a = np.empty((k // 512, 16))
    for p in range(k // 512):
        a[p, :8] = np.random.permutation(np.resize(levels, 8))
        for g in range(8):
            far = levels[np.abs(levels - a[p, g]) >= 10]
            a[p, g + 8] = far[np.random.randint(len(far))]
    return np.exp2(a.ravel()).repeat(32)


def f64(x):
    return np.asarray(x).astype(np.float64)


def striped(idx):
    return np.tile(idx.reshape(-1, 16).T, (8, 1)).astype(np.uint16)


def unstriped(offs):
    return offs[:16].T.reshape(-1).astype(np.int64)


def striped8(idx):
    return np.concatenate([x.reshape(-1, 16).T for x in idx]).astype(np.uint16)


def runs(offs, k):
    lists = np.stack([offs[16 * r : 16 * r + 16].T.reshape(-1) for r in range(8)]).astype(np.int64)
    return lists[np.arange(k) % 512 // 64]


def pack_weight(w):
    k, n = w.shape
    w = f64(np.asarray(w, np.float32).astype(ml_dtypes.bfloat16)).reshape(k // 32, 32, n)
    amax = np.abs(w).max(1)
    byte = np.clip(np.where(amax > 0, np.frexp(amax)[1] - 1 + 127 - 7, 1), 1, 254)
    scaled = (w * np.exp2(127.0 - byte)[:, None, :]).reshape(k, n).astype(np.float32)
    words = np.ascontiguousarray(scaled.reshape(k // 512, 128, 4, n).transpose(0, 1, 3, 2)).astype(ml_dtypes.float8_e4m3fn).view(np.uint8)
    return words, np.ascontiguousarray(byte.astype(np.uint8).reshape(k // 512, 16, n))


def unpack_weight(words, scales):
    g, p, n, _ = words.shape
    vals = np.ascontiguousarray(words).view(ml_dtypes.float8_e4m3fn).astype(np.float64) * np.repeat(np.exp2(scales.astype(np.float64) - 127.0), 8, axis=1)[..., None]
    return vals.transpose(0, 1, 3, 2).reshape(g * 512, n)


E2M1 = np.array([0.0, 0.5, 1.0, 1.5, 2.0, 3.0, 4.0, 6.0, -0.0, -0.5, -1.0, -1.5, -2.0, -3.0, -4.0, -6.0])


def pack_fp4(w):
    k, n = w.shape
    w = f64(np.asarray(w, np.float32).astype(ml_dtypes.bfloat16)).reshape(k // 32, 32, n)
    amax = np.abs(w).max(1)
    mant, ex = np.frexp(amax / 6.0)
    byte = np.clip(np.where(amax > 0, np.where(mant > 0.5, ex, ex - 1) + 127, 1), 1, 254)
    scaled = (w * np.exp2(127.0 - byte)[:, None, :]).reshape(k, n).astype(np.float32)
    c = np.ascontiguousarray(scaled.reshape(k // 512, 128, 4, n).transpose(0, 1, 3, 2)).astype(ml_dtypes.float4_e2m1fn).view(np.uint8) & 0xF
    words = (c[..., 0::2] | (c[..., 1::2] << 4)).reshape(k // 512, 128, 2 * n)
    return np.ascontiguousarray(words), np.ascontiguousarray(byte.astype(np.uint8).reshape(k // 512, 16, n))


def unpack_fp4(words, scales):
    g, _, n = scales.shape
    words = np.ascontiguousarray(words).reshape(g, 128, n, 2)
    nib = np.empty((g, 128, n, 4), np.uint8)
    nib[..., 0::2] = words & 0xF
    nib[..., 1::2] = words >> 4
    vals = E2M1[nib] * np.repeat(np.exp2(scales.astype(np.float64) - 127.0), 8, axis=1)[..., None]
    return vals.transpose(0, 1, 3, 2).reshape(g * 512, n)


def sigmoid(v):
    return 1.0 / (1.0 + np.exp(-np.maximum(v, -700.0)))


K, T, S, N, G, H, U = 512, 1024, 256, 512, 2048, 512, 512


def setup_inputs():
    n = np.random.standard_normal
    s = mx_kscale(K)[:, None]
    u = mx_kscale(K)
    packed_xT = pack_weight(n((K, T)) * s)
    packed_dT = pack_weight(n((K, G)) / s)
    packed_w1 = pack_fp4(n((H, N)) / np.sqrt(H) / u[:, None])
    perm = np.random.permutation(U)
    return {
        "x_words": packed_xT[0],
        "x_scales": packed_xT[1],
        "d_words": packed_dT[0],
        "d_scales": packed_dT[1],
        "sl": np.random.uniform(1.0, 2.0, (H, 1)).astype(np.float32),
        "th": (0.5 * n((H, 1))).astype(np.float32),
        "gn": (np.random.uniform(0.5, 1.5, (H, 1)) * u[:, None]).astype(np.float32),
        "w1_words": packed_w1[0],
        "w1_scales": packed_w1[1],
        "offs": striped(np.random.permutation(T)[:S]),
        "ka": striped8(np.random.randint(0, G, (8, H))),
        "kb": striped8(np.random.randint(0, G, (8, H))),
        "n1": striped8(np.stack([np.random.permutation(S) for _ in range(8)])),
        "n2": striped8(np.stack([np.random.permutation(S) for _ in range(8)])),
        "n3": striped(perm[:S]),
        "n4": striped(perm[S:]),
        "n5": striped(np.random.permutation(S)),
    }


def reference(x_words, x_scales, d_words, d_scales, sl, th, gn, w1_words, w1_scales, offs, ka, kb, n1, n2, n3, n4, n5):
    d_ka = unpack_weight(d_words, d_scales)[np.arange(K)[:, None], runs(ka, K)]
    xq = unpack_weight(x_words, x_scales)[:, unstriped(offs)]
    d_kb = unpack_weight(d_words, d_scales)[np.arange(K)[:, None], runs(kb, K)]
    h = 0.0625 * (d_ka.T @ xq + d_kb.T @ xq)
    st = np.maximum(h, h[np.arange(H)[:, None], runs(n1, H)])
    sg = sigmoid(f64(sl) * (st[np.arange(H)[:, None], runs(n2, H)] - f64(th)))
    z = f64(gn) * (st * sg)
    h2 = unpack_fp4(w1_words, w1_scales).T @ mxq(z, 0, "e4m3")
    dn = np.minimum(h2, h2[:, unstriped(n5)])
    up = np.maximum(h2, h2[:, unstriped(n5)])
    ph = np.zeros((N, U))
    ph[:, unstriped(n3)] = up
    out = ph.copy()
    out[:, unstriped(n4)] = dn
    return out

@@ -1,0 +1,212 @@
+from contextlib import ExitStack
+
+import concourse.mybir as mybir
+
+K, T, S, N, G, H, U = 512, 1024, 256, 512, 2048, 512, 512
+FLOPS = 2 * (2 * K * H * S + H * N * S)
+
+F32 = mybir.dt.float32
+BF16 = mybir.dt.bfloat16
+I32 = mybir.dt.int32
+U32 = mybir.dt.uint32
+U16 = mybir.dt.uint16
+U8 = mybir.dt.uint8
+FP8X4 = mybir.dt.float8_e4m3fn_x4
+FP4X4 = mybir.dt.float4_e2m1fn_x4
+ACT = mybir.ActivationFunctionType
+ALU = mybir.AluOpType
+
+P = 128
+PACK = 4
+HALF = S // 2
+
+
+def tile_picked_aqlehhpagmx_none_p_kernel(
+    tc, x_words, x_scales, d_words, d_scales, sl, th, gn, w1_words, w1_scales, offs, ka, kb, n1, n2, n3, n4, n5, out
+):
+    nc = tc.nc
+    with ExitStack() as ctx:
+        sb = ctx.enter_context(tc.tile_pool(name="sb", bufs=1))
+        psum = ctx.enter_context(tc.psum_pool(name="psum", bufs=1))
+
+        def load_list(src, name):
+            tile = sb.tile([P, src.shape[1]], U16, name=name)
+            nc.sync.dma_start(tile[:], src)
+            return tile
+
+        def load_scale_window(scales, name):
+            cols = scales.shape[2]
+            tile = sb.tile([P, cols], U8, name=name, align_bytes=64)
+            rows = scales[0].bitcast(I32)
+            nc.scalar.dma_start(tile[:].bitcast(I32), rows.unsqueeze(1).to_broadcast([16, 8, cols // 4]))
+            return tile
+
+        def load_word_window(words, name):
+            tile = sb.tile([P, words.shape[2]], U32, name=name, align_bytes=64)
+            nc.scalar.dma_start(tile[:].bitcast(I32), words[0].rearrange("p n t -> p (n t)").bitcast(I32))
+            return tile
+
+        kb_l = load_list(kb, "kb_l")
+        d_sc_win = load_scale_window(d_scales, "d_sc_win")
+        ka_l = load_list(ka, "ka_l")
+        x_sc_win = load_scale_window(x_scales, "x_sc_win")
+        offs_l = load_list(offs, "offs_l")
+        d_w_win = load_word_window(d_words, "d_w_win")
+        x_w_win = load_word_window(x_words, "x_w_win")
+        n1_l = load_list(n1, "n1_l")
+        n2_l = load_list(n2, "n2_l")
+        n5_l = load_list(n5, "n5_l")
+        n3_l = load_list(n3, "n3_l")
+        n4_l = load_list(n4, "n4_l")
+
+        def load_column(src, name):
+            tile = sb.tile([P, PACK], F32, name=name)
+            nc.gpsimd.dma_start(tile[:], src.rearrange("(p t) o -> p (t o)", t=PACK))
+            return tile
+
+        sl_t = load_column(sl, "sl_t")
+        th_t = load_column(th, "th_t")
+        gn_t = load_column(gn, "gn_t")
+
+        planes = sb.tile([P, H + S], U8, name="planes", align_bytes=64)
+        nc.vector.memset(planes[:].bitcast(I32), 0)
+
+        sc_b = sb.tile([P, H], U8, name="sc_b", tag="b_then_w1_words", align_bytes=64)
+        sc_ax = sb.tile([P, H + S], U8, name="sc_ax", tag="ax_then_w1_scales", align_bytes=64)
+        nc.vector.tensor_copy(sc_b[:], d_sc_win[:].indirect(kb_l[:]))
+        for i in range(4):
+            nc.sync.dma_start(planes[4 + i : P : 32, 0:H].bitcast(I32), sc_b[8 * i : P : 32, :].bitcast(I32))
+        nc.vector.tensor_copy(sc_ax[:, 0:H], d_sc_win[:].indirect(ka_l[:]))
+        nc.vector.tensor_copy(sc_ax[:, H : H + S], x_sc_win[:].indirect(offs_l[:]))
+        for i in range(4):
+            nc.scalar.dma_start(planes[i:P:32, :].bitcast(I32), sc_ax[8 * i : P : 32, :].bitcast(I32))
+
+        w1_w = sb.tile([P, 2 * N], U8, name="w1_w", tag="b_then_w1_words", align_bytes=64)
+        w1_sc = sb.tile([P, N], U8, name="w1_sc", tag="ax_then_w1_scales", align_bytes=64)
+        nc.gpsimd.memset(w1_sc[:].bitcast(I32), 0)
+        nc.sync.dma_start(w1_w[:].bitcast(I32), w1_words[0].bitcast(I32))
+        for q in range(4):
+            nc.sync.dma_start(w1_sc[32 * q : 32 * q + 4, :].bitcast(I32), w1_scales[0, 4 * q : 4 * q + 4, :].bitcast(I32))
+
+
+        def gather_and_deal(lst, name):
+            got = sb.tile([P, H], U32, name=name + "_got", align_bytes=64)
+            nc.vector.tensor_copy(got[:], d_w_win[:].indirect(lst[:]))
+            dealt = sb.tile([P, H], U32, name=name + "_dealt", align_bytes=64)
+            nc.vector.tensor_copy(
+                dealt[:].bitcast(I32).rearrange("p (t m) -> p m t", t=PACK),
+                got[:].bitcast(I32).rearrange("p (m t) -> p m t", t=PACK),
+            )
+            return dealt
+
+        wa = gather_and_deal(ka_l, "wa")
+        wb = gather_and_deal(kb_l, "wb")
+        xq = sb.tile([P, S], U32, name="xq", align_bytes=64)
+        nc.vector.tensor_copy(xq[:], x_w_win[:].indirect(offs_l[:]))
+        d_planes = sb.tile([P, H], U8, name="d_planes", align_bytes=64)
+        nc.vector.tensor_copy(
+            d_planes[:].rearrange("p (t m) -> p m t", t=PACK),
+            planes[:, 0:H].rearrange("p (m t) -> p m t", t=PACK),
+        )
+
+        bias = sb.tile([P, PACK], F32, name="bias")
+        nc.vector.scalar_tensor_tensor(bias[:], sl_t[:], -1.0, th_t[:], ALU.mult, ALU.mult)
+
+        h_t = []
+        for t in range(PACK):
+            cols = slice(P * t, P * (t + 1))
+            acc = psum.tile([P, S], F32, name=f"acc_h{t}", tag=f"bank{t}")
+            nc.tensor.matmul_mx(acc[:], lhsT=wa[:, cols].bitcast(FP8X4), lhsT_scale=d_planes[:, cols],
+                                rhs=xq[:].bitcast(FP8X4), rhs_scale=planes[:, H : H + S], start=True, stop=False)
+            nc.tensor.matmul_mx(acc[:], lhsT=wb[:, cols].bitcast(FP8X4), lhsT_scale=d_planes[4:P, cols],
+                                rhs=xq[:].bitcast(FP8X4), rhs_scale=planes[:, H : H + S], start=False, stop=True)
+            h = sb.tile([P, S], F32, name=f"h{t}", tag=f"h{t}")
+            nc.vector.tensor_scalar(h[:], acc[:], 0.0625, None, ALU.mult)
+            h_t.append(h)
+
+        def gather(dst, window, lst, lo, hi, func=ACT.Copy, **kw):
+            nc.scalar.activation(dst[:, lo:hi], window[:].indirect(lst[:, lo // 16 : hi // 16]), func, **kw)
+
+        st_t = []
+        u = sb.tile([P, PACK, S], F32, name="u")
+        for t in range(PACK):
+            g1 = sb.tile([P, S], F32, name=f"g1_{t}", tag=f"g1_{t}")
+            for c in range(2):
+                gather(g1, h_t[t], n1_l, c * HALF, (c + 1) * HALF)
+            st = sb.tile([P, S], F32, name=f"st{t}")
+            nc.vector.tensor_tensor(st[:], h_t[t][:], g1[:], ALU.max)
+            nc.vector.tensor_scalar(u[:, t, :], st[:], gn_t[:, t : t + 1], None, ALU.mult)
+            st_t.append(st)
+
+        zi = sb.tile([P, S, PACK], BF16, name="zi", align_bytes=64)
+        z_codes = sb.tile([P, S], U32, name="z_codes", align_bytes=64)
+        z_sc = sb.tile([P, S], U8, name="z_sc", align_bytes=64)
+
+        def make_z(lo, hi, tag):
+            sg = sb.tile([P, PACK, hi - lo], F32, name=f"sg{lo}", tag=tag)
+            for t in range(PACK):
+                nc.scalar.activation(sg[:, t, :], st_t[t][:].indirect(n2_l[:, lo // 16 : hi // 16]), ACT.Sigmoid,
+                                     bias=bias[:, t : t + 1], scale=sl_t[:, t : t + 1])
+            nc.vector.tensor_tensor(
+                zi[:, lo:hi, :].rearrange("p (c i) t -> p c t i", i=4),
+                u[:, :, lo:hi].rearrange("p t (c i) -> p c t i", i=4),
+                sg[:].rearrange("p t (c i) -> p c t i", i=4),
+                ALU.mult,
+            )
+
+        def quantise(lo, hi):
+            nc.vector.quantize_mx(z_codes[:, lo:hi].bitcast(FP8X4), z_sc[:, lo:hi], zi[:, lo:hi, :].rearrange("p c t -> p (c t)"))
+
+        h2_t = [sb.tile([P, S], F32, name=f"h2_{m}") for m in range(4)]
+
+        def second_product(m, lo, hi, bank):
+            acc = psum.tile([P, hi - lo], F32, name=f"acc_o{m}_{lo}", tag=f"bank{bank}")
+            nc.tensor.matmul_mx(acc[:], lhsT=w1_w[:, 2 * P * m : 2 * P * (m + 1)].bitcast(FP4X4),
+                                lhsT_scale=w1_sc[:, P * m : P * (m + 1)],
+                                rhs=z_codes[:, lo:hi].bitcast(FP8X4), rhs_scale=z_sc[:, lo:hi], start=True, stop=True)
+            nc.vector.tensor_copy(h2_t[m][:, lo:hi], acc[:])
+
+        make_z(0, HALF, "sg")
+        quantise(0, HALF)
+        second_product(0, 0, HALF, 4)
+        make_z(HALF, HALF + 64, "g1_3")
+        make_z(HALF + 64, S, "h3")
+        quantise(HALF, S)
+        second_product(0, HALF, S, 5)
+        for m in range(1, 4):
+            second_product(m, 0, S, (5 + m) % 8)
+
+        up_t, dn_t, pages = [], [], []
+
+        def fetch(m):
+            g5 = sb.tile([P, S], F32, name=f"g5_{m}")
+            for c in range(2):
+                gather(g5, h2_t[m], n5_l, c * HALF, (c + 1) * HALF)
+            up = sb.tile([P, S], F32, name=f"up{m}")
+            nc.vector.tensor_tensor(up[:], h2_t[m][:], g5[:], ALU.max)
+            dn = sb.tile([P, S], F32, name=f"dn{m}")
+            nc.vector.tensor_tensor(dn[:], h2_t[m][:], g5[:], ALU.min)
+            up_t.append(up)
+            dn_t.append(dn)
+
+        def put_up(m):
+            page = sb.tile([P, U], F32, name=f"page{m}")
+            pages.append(page)
+            nc.scalar.activation(page[:].indirect(n3_l[:]), up_t[m][:], ACT.Copy)
+
+        def put_dn(m):
+            nc.scalar.activation(pages[m][:].indirect(n4_l[:]), dn_t[m][:], ACT.Copy)
+            nc.sync.dma_start(out[P * m : P * (m + 1), :], pages[m][:])
+
+        fetch(0)
+        fetch(1)
+        put_up(0)
+        fetch(2)
+        put_up(1)
+        fetch(3)
+        put_dn(0)
+        put_up(2)
+        put_dn(1)
+        put_up(3)
+        put_dn(2)
+        put_dn(3)

@@ -36,21 +36,21 @@ def tile_picked_aqlehhpagmx_none_p_kernel(
 
         def load_scale_window(scales, name):
             cols = scales.shape[2]
-            tile = sb.tile([P, cols], U8, name=name, align_bytes=64)
+            tile = sb.tile([P, cols], U8, name=name, tag=name, align_bytes=64)
             rows = scales[0].bitcast(I32)
             nc.scalar.dma_start(tile[:].bitcast(I32), rows.unsqueeze(1).to_broadcast([16, 8, cols // 4]))
             return tile
 
         def load_word_window(words, name):
-            tile = sb.tile([P, words.shape[2]], U32, name=name, align_bytes=64)
+            tile = sb.tile([P, words.shape[2]], U32, name=name, tag=name, align_bytes=64)
             nc.scalar.dma_start(tile[:].bitcast(I32), words[0].rearrange("p n t -> p (n t)").bitcast(I32))
             return tile
 
-        kb_l = load_list(kb, "kb_l")
-        d_sc_win = load_scale_window(d_scales, "d_sc_win")
-        ka_l = load_list(ka, "ka_l")
-        x_sc_win = load_scale_window(x_scales, "x_sc_win")
         offs_l = load_list(offs, "offs_l")
+        x_sc_win = load_scale_window(x_scales, "x_sc_win")
+        ka_l = load_list(ka, "ka_l")
+        d_sc_win = load_scale_window(d_scales, "d_sc_win")
+        kb_l = load_list(kb, "kb_l")
         d_w_win = load_word_window(d_words, "d_w_win")
         x_w_win = load_word_window(x_words, "x_w_win")
         n1_l = load_list(n1, "n1_l")
@@ -67,97 +67,104 @@ def tile_picked_aqlehhpagmx_none_p_kernel(
         sl_t = load_column(sl, "sl_t")
         th_t = load_column(th, "th_t")
         gn_t = load_column(gn, "gn_t")
+        sl_th = sb.tile([P, PACK], F32, name="sl_th")
+        nc.gpsimd.tensor_tensor(sl_th[:], sl_t[:], th_t[:], ALU.mult)
+        bias = sb.tile([P, PACK], F32, name="bias")
+        nc.gpsimd.tensor_scalar(bias[:], sl_th[:], -1.0, 0.0, ALU.mult, ALU.add)
 
         planes = sb.tile([P, H + S], U8, name="planes", align_bytes=64)
         nc.vector.memset(planes[:].bitcast(I32), 0)
 
-        sc_b = sb.tile([P, H], U8, name="sc_b", tag="b_then_w1_words", align_bytes=64)
-        sc_ax = sb.tile([P, H + S], U8, name="sc_ax", tag="ax_then_w1_scales", align_bytes=64)
+        def window(name, width):
+            tile = sb.tile([P, width], F32, name=name, tag=name)
+            nc.vector.memset(tile[:, S:width], 0.0)
+            return tile
+
+        h_t = [window(f"h{t}", 2 * S) for t in range(PACK)]
+        st_t = [sb.tile([P, S], F32, name=f"st{t}") for t in range(PACK)]
+        h2_t = [window(f"h2_{m}", S + 16) for m in range(4)]
+
+        warm = sb.tile([P, 1], F32, name="warm")
+        nc.scalar.activation(warm[:], h_t[0][:, S : S + 1], ACT.Sigmoid)
+
+        sc_b = sb.tile([P, H], U8, name="sc_b", tag="sc_b", align_bytes=64)
+        sc_ax = sb.tile([P, H + S], U8, name="sc_ax", tag="sc_ax", align_bytes=64)
+        nc.vector.tensor_copy(sc_ax[:, H : H + S], x_sc_win[:].indirect(offs_l[:]))
+        nc.vector.tensor_copy(sc_ax[:, 0:H], d_sc_win[:].indirect(ka_l[:]))
+        for i in range(4):
+            nc.sync.dma_start(planes[i:P:32, :].bitcast(I32), sc_ax[8 * i : P : 32, :].bitcast(I32))
         nc.vector.tensor_copy(sc_b[:], d_sc_win[:].indirect(kb_l[:]))
         for i in range(4):
-            nc.sync.dma_start(planes[4 + i : P : 32, 0:H].bitcast(I32), sc_b[8 * i : P : 32, :].bitcast(I32))
-        nc.vector.tensor_copy(sc_ax[:, 0:H], d_sc_win[:].indirect(ka_l[:]))
-        nc.vector.tensor_copy(sc_ax[:, H : H + S], x_sc_win[:].indirect(offs_l[:]))
-        for i in range(4):
-            nc.scalar.dma_start(planes[i:P:32, :].bitcast(I32), sc_ax[8 * i : P : 32, :].bitcast(I32))
+            nc.scalar.dma_start(planes[4 + i : P : 32, 0:H].bitcast(I32), sc_b[8 * i : P : 32, :].bitcast(I32))
 
-        w1_w = sb.tile([P, 2 * N], U8, name="w1_w", tag="b_then_w1_words", align_bytes=64)
-        w1_sc = sb.tile([P, N], U8, name="w1_sc", tag="ax_then_w1_scales", align_bytes=64)
+        words = sb.tile([P, 2 * H + S], U32, name="words", tag="d_sc_win", align_bytes=64)
+        xq = words[:, 2 * H : 2 * H + S]
+
+        nc.vector.tensor_copy(words[:, 0:H], d_w_win[:].indirect(ka_l[:]))
+        nc.vector.tensor_copy(words[:, H : 2 * H], d_w_win[:].indirect(kb_l[:]))
+        nc.vector.tensor_copy(xq, x_w_win[:].indirect(offs_l[:]))
+
+        got_w = words[:, 0 : 2 * H].bitcast(I32).rearrange("p (l m t) -> p l m t", l=2, t=PACK)
+        got_p = planes[:, 0:H].rearrange("p (m t) -> p m t", t=PACK)
+
+        def deal_words(name, t0, t1):
+            dst = sb.tile([P, 2, t1 - t0, P], U32, name=name, tag=name, align_bytes=64)
+            nc.vector.tensor_copy(dst[:].bitcast(I32).rearrange("p l t m -> p l m t"), got_w[:, :, :, t0:t1])
+            return [dst[:, :, k, :] for k in range(t1 - t0)]
+
+        def deal_planes(name, t0, t1):
+            dst = sb.tile([P, t1 - t0, P], U8, name=name, align_bytes=64)
+            nc.vector.tensor_copy(dst[:].rearrange("p t m -> p m t"), got_p[:, :, t0:t1])
+            return [dst[:, k, :] for k in range(t1 - t0)]
+
+        d_w = deal_words("w_first", 0, 1)
+        d_planes = deal_planes("planes_first", 0, 1)
+        d_w = d_w + deal_words("sc_b", 1, PACK)
+        d_planes = d_planes + deal_planes("planes_rest", 1, PACK)
+
+        w1_w = sb.tile([P, 2 * N], U8, name="w1_w", tag="x_w_win", align_bytes=64)
+        w1_sc = sb.tile([P, N], U8, name="w1_sc", tag="d_w_win", align_bytes=64)
         nc.gpsimd.memset(w1_sc[:].bitcast(I32), 0)
         nc.sync.dma_start(w1_w[:].bitcast(I32), w1_words[0].bitcast(I32))
         for q in range(4):
             nc.sync.dma_start(w1_sc[32 * q : 32 * q + 4, :].bitcast(I32), w1_scales[0, 4 * q : 4 * q + 4, :].bitcast(I32))
 
-
-        def gather_and_deal(lst, name):
-            got = sb.tile([P, H], U32, name=name + "_got", align_bytes=64)
-            nc.vector.tensor_copy(got[:], d_w_win[:].indirect(lst[:]))
-            dealt = sb.tile([P, H], U32, name=name + "_dealt", align_bytes=64)
-            nc.vector.tensor_copy(
-                dealt[:].bitcast(I32).rearrange("p (t m) -> p m t", t=PACK),
-                got[:].bitcast(I32).rearrange("p (m t) -> p m t", t=PACK),
-            )
-            return dealt
-
-        wa = gather_and_deal(ka_l, "wa")
-        wb = gather_and_deal(kb_l, "wb")
-        xq = sb.tile([P, S], U32, name="xq", align_bytes=64)
-        nc.vector.tensor_copy(xq[:], x_w_win[:].indirect(offs_l[:]))
-        d_planes = sb.tile([P, H], U8, name="d_planes", align_bytes=64)
-        nc.vector.tensor_copy(
-            d_planes[:].rearrange("p (t m) -> p m t", t=PACK),
-            planes[:, 0:H].rearrange("p (m t) -> p m t", t=PACK),
-        )
-
-        bias = sb.tile([P, PACK], F32, name="bias")
-        nc.vector.scalar_tensor_tensor(bias[:], sl_t[:], -1.0, th_t[:], ALU.mult, ALU.mult)
-
-        h_t = []
         for t in range(PACK):
-            cols = slice(P * t, P * (t + 1))
             acc = psum.tile([P, S], F32, name=f"acc_h{t}", tag=f"bank{t}")
-            nc.tensor.matmul_mx(acc[:], lhsT=wa[:, cols].bitcast(FP8X4), lhsT_scale=d_planes[:, cols],
-                                rhs=xq[:].bitcast(FP8X4), rhs_scale=planes[:, H : H + S], start=True, stop=False)
-            nc.tensor.matmul_mx(acc[:], lhsT=wb[:, cols].bitcast(FP8X4), lhsT_scale=d_planes[4:P, cols],
-                                rhs=xq[:].bitcast(FP8X4), rhs_scale=planes[:, H : H + S], start=False, stop=True)
-            h = sb.tile([P, S], F32, name=f"h{t}", tag=f"h{t}")
-            nc.vector.tensor_scalar(h[:], acc[:], 0.0625, None, ALU.mult)
-            h_t.append(h)
+            nc.tensor.matmul_mx(acc[:], lhsT=d_w[t][:, 0, :].bitcast(FP8X4), lhsT_scale=d_planes[t],
+                                rhs=xq.bitcast(FP8X4), rhs_scale=planes[:, H : H + S], start=True, stop=False)
+            nc.tensor.matmul_mx(acc[:], lhsT=d_w[t][:, 1, :].bitcast(FP8X4), lhsT_scale=d_planes[t][4:P, :],
+                                rhs=xq.bitcast(FP8X4), rhs_scale=planes[:, H : H + S], start=False, stop=True)
+            if t == 0:
+                nc.scalar.activation(h_t[t][:, 0:S], acc[:], ACT.Copy, scale=0.0625)
+            else:
+                nc.vector.tensor_scalar(h_t[t][:, 0:S], acc[:], 0.0625, None, ALU.mult)
 
-        def gather(dst, window, lst, lo, hi, func=ACT.Copy, **kw):
-            nc.scalar.activation(dst[:, lo:hi], window[:].indirect(lst[:, lo // 16 : hi // 16]), func, **kw)
-
-        st_t = []
-        u = sb.tile([P, PACK, S], F32, name="u")
         for t in range(PACK):
             g1 = sb.tile([P, S], F32, name=f"g1_{t}", tag=f"g1_{t}")
-            for c in range(2):
-                gather(g1, h_t[t], n1_l, c * HALF, (c + 1) * HALF)
-            st = sb.tile([P, S], F32, name=f"st{t}")
-            nc.vector.tensor_tensor(st[:], h_t[t][:], g1[:], ALU.max)
-            nc.vector.tensor_scalar(u[:, t, :], st[:], gn_t[:, t : t + 1], None, ALU.mult)
-            st_t.append(st)
+            nc.scalar.activation(g1[:], h_t[t][:].indirect(n1_l[:]), ACT.Copy)
+            nc.vector.tensor_tensor(st_t[t][:, 0:S], h_t[t][:, 0:S], g1[:], ALU.max)
+        u = sb.tile([P, PACK, S], F32, name="u", tag="h2")
+        for t in range(PACK):
+            nc.vector.tensor_scalar(u[:, t, :], st_t[t][:], gn_t[:, t : t + 1], None, ALU.mult)
 
-        zi = sb.tile([P, S, PACK], BF16, name="zi", align_bytes=64)
         z_codes = sb.tile([P, S], U32, name="z_codes", align_bytes=64)
         z_sc = sb.tile([P, S], U8, name="z_sc", align_bytes=64)
 
-        def make_z(lo, hi, tag):
+        def make_z(zi, lo, hi, tag):
             sg = sb.tile([P, PACK, hi - lo], F32, name=f"sg{lo}", tag=tag)
             for t in range(PACK):
                 nc.scalar.activation(sg[:, t, :], st_t[t][:].indirect(n2_l[:, lo // 16 : hi // 16]), ACT.Sigmoid,
                                      bias=bias[:, t : t + 1], scale=sl_t[:, t : t + 1])
             nc.vector.tensor_tensor(
-                zi[:, lo:hi, :].rearrange("p (c i) t -> p c t i", i=4),
+                zi[:, lo % HALF : lo % HALF + hi - lo, :].rearrange("p (c i) t -> p c t i", i=4),
                 u[:, :, lo:hi].rearrange("p t (c i) -> p c t i", i=4),
                 sg[:].rearrange("p t (c i) -> p c t i", i=4),
                 ALU.mult,
             )
 
-        def quantise(lo, hi):
-            nc.vector.quantize_mx(z_codes[:, lo:hi].bitcast(FP8X4), z_sc[:, lo:hi], zi[:, lo:hi, :].rearrange("p c t -> p (c t)"))
-
-        h2_t = [sb.tile([P, S], F32, name=f"h2_{m}") for m in range(4)]
+        def quantise(zi, lo, hi):
+            nc.vector.quantize_mx(z_codes[:, lo:hi].bitcast(FP8X4), z_sc[:, lo:hi], zi[:].rearrange("p c t -> p (c t)"))
 
         def second_product(m, lo, hi, bank):
             acc = psum.tile([P, hi - lo], F32, name=f"acc_o{m}_{lo}", tag=f"bank{bank}")
@@ -166,47 +173,31 @@ def tile_picked_aqlehhpagmx_none_p_kernel(
                                 rhs=z_codes[:, lo:hi].bitcast(FP8X4), rhs_scale=z_sc[:, lo:hi], start=True, stop=True)
             nc.vector.tensor_copy(h2_t[m][:, lo:hi], acc[:])
 
-        make_z(0, HALF, "sg")
-        quantise(0, HALF)
+        z_first = sb.tile([P, HALF, PACK], BF16, name="z_first", tag="z_half", align_bytes=64)
+        make_z(z_first, 0, HALF, "g1_2")
+        quantise(z_first, 0, HALF)
         second_product(0, 0, HALF, 4)
-        make_z(HALF, HALF + 64, "g1_3")
-        make_z(HALF + 64, S, "h3")
-        quantise(HALF, S)
+        z_second = sb.tile([P, HALF, PACK], BF16, name="z_second", tag="z_half", align_bytes=64)
+        make_z(z_second, HALF, HALF + 64, "g1_3")
+        make_z(z_second, HALF + 64, S, "h3")
+        quantise(z_second, HALF, S)
         second_product(0, HALF, S, 5)
         for m in range(1, 4):
             second_product(m, 0, S, (5 + m) % 8)
 
-        up_t, dn_t, pages = [], [], []
-
-        def fetch(m):
+        g5_t, pages = [], []
+        for m in range(4):
             g5 = sb.tile([P, S], F32, name=f"g5_{m}")
-            for c in range(2):
-                gather(g5, h2_t[m], n5_l, c * HALF, (c + 1) * HALF)
-            up = sb.tile([P, S], F32, name=f"up{m}")
-            nc.vector.tensor_tensor(up[:], h2_t[m][:], g5[:], ALU.max)
-            dn = sb.tile([P, S], F32, name=f"dn{m}")
-            nc.vector.tensor_tensor(dn[:], h2_t[m][:], g5[:], ALU.min)
-            up_t.append(up)
-            dn_t.append(dn)
-
-        def put_up(m):
+            nc.scalar.activation(g5[:], h2_t[m][:].indirect(n5_l[:]), ACT.Copy)
+            g5_t.append(g5)
+        for m in range(4):
+            up = sb.tile([P, S], F32, name=f"up{m}", tag=f"put{m}")
+            nc.vector.tensor_tensor(up[:], h2_t[m][:, 0:S], g5_t[m][:], ALU.max)
             page = sb.tile([P, U], F32, name=f"page{m}")
+            nc.scalar.activation(page[:].indirect(n3_l[:]), up[:], ACT.Copy)
             pages.append(page)
-            nc.scalar.activation(page[:].indirect(n3_l[:]), up_t[m][:], ACT.Copy)
-
-        def put_dn(m):
-            nc.scalar.activation(pages[m][:].indirect(n4_l[:]), dn_t[m][:], ACT.Copy)
+        for m in range(4):
+            dn = sb.tile([P, S], F32, name=f"dn{m}", tag=f"put{m}")
+            nc.vector.tensor_tensor(dn[:], h2_t[m][:, 0:S], g5_t[m][:], ALU.min)
+            nc.scalar.activation(pages[m][:].indirect(n4_l[:]), dn[:], ACT.Copy)
             nc.sync.dma_start(out[P * m : P * (m + 1), :], pages[m][:])
-
-        fetch(0)
-        fetch(1)
-        put_up(0)
-        fetch(2)
-        put_up(1)
-        fetch(3)
-        put_dn(0)
-        put_up(2)
-        put_dn(1)
-        put_up(3)
-        put_dn(2)
-        put_dn(3)

@@ -144,27 +144,27 @@ def tile_picked_aqlehhpagmx_none_p_kernel(
             g1 = sb.tile([P, S], F32, name=f"g1_{t}", tag=f"g1_{t}")
             nc.scalar.activation(g1[:], h_t[t][:].indirect(n1_l[:]), ACT.Copy)
             nc.vector.tensor_tensor(st_t[t][:, 0:S], h_t[t][:, 0:S], g1[:], ALU.max)
-        u = sb.tile([P, PACK, S], F32, name="u", tag="h2")
+        u = sb.tile([P, PACK, S], F32, name="u", tag="h3")
         for t in range(PACK):
             nc.vector.tensor_scalar(u[:, t, :], st_t[t][:], gn_t[:, t : t + 1], None, ALU.mult)
 
+        zi = sb.tile([P, S, PACK], BF16, name="zi", align_bytes=64)
         z_codes = sb.tile([P, S], U32, name="z_codes", align_bytes=64)
         z_sc = sb.tile([P, S], U8, name="z_sc", align_bytes=64)
 
-        def make_z(zi, lo, hi, tag):
-            sg = sb.tile([P, PACK, hi - lo], F32, name=f"sg{lo}", tag=tag)
+        def make_z(sg, lo, hi):
             for t in range(PACK):
                 nc.scalar.activation(sg[:, t, :], st_t[t][:].indirect(n2_l[:, lo // 16 : hi // 16]), ACT.Sigmoid,
                                      bias=bias[:, t : t + 1], scale=sl_t[:, t : t + 1])
             nc.vector.tensor_tensor(
-                zi[:, lo % HALF : lo % HALF + hi - lo, :].rearrange("p (c i) t -> p c t i", i=4),
+                zi[:, lo:hi, :].rearrange("p (c i) t -> p c t i", i=4),
                 u[:, :, lo:hi].rearrange("p t (c i) -> p c t i", i=4),
-                sg[:].rearrange("p t (c i) -> p c t i", i=4),
+                sg.rearrange("p t (c i) -> p c t i", i=4),
                 ALU.mult,
             )
 
-        def quantise(zi, lo, hi):
-            nc.vector.quantize_mx(z_codes[:, lo:hi].bitcast(FP8X4), z_sc[:, lo:hi], zi[:].rearrange("p c t -> p (c t)"))
+        def quantise(lo, hi):
+            nc.vector.quantize_mx(z_codes[:, lo:hi].bitcast(FP8X4), z_sc[:, lo:hi], zi[:, lo:hi, :].rearrange("p c t -> p (c t)"))
 
         def second_product(m, lo, hi, bank):
             acc = psum.tile([P, hi - lo], F32, name=f"acc_o{m}_{lo}", tag=f"bank{bank}")
@@ -173,14 +173,14 @@ def tile_picked_aqlehhpagmx_none_p_kernel(
                                 rhs=z_codes[:, lo:hi].bitcast(FP8X4), rhs_scale=z_sc[:, lo:hi], start=True, stop=True)
             nc.vector.tensor_copy(h2_t[m][:, lo:hi], acc[:])
 
-        z_first = sb.tile([P, HALF, PACK], BF16, name="z_first", tag="z_half", align_bytes=64)
-        make_z(z_first, 0, HALF, "g1_2")
-        quantise(z_first, 0, HALF)
+        sg_half = sb.tile([P, PACK, HALF], F32, name="sg_half", tag="g1_2")
+        sg_quarters = sb.tile([P, 2, PACK, HALF // 2], F32, name="sg_quarters", tag="g1_3")
+        make_z(sg_half[:], 0, HALF)
+        quantise(0, HALF)
         second_product(0, 0, HALF, 4)
-        z_second = sb.tile([P, HALF, PACK], BF16, name="z_second", tag="z_half", align_bytes=64)
-        make_z(z_second, HALF, HALF + 64, "g1_3")
-        make_z(z_second, HALF + 64, S, "h3")
-        quantise(z_second, HALF, S)
+        make_z(sg_quarters[:, 0, :, :], HALF, HALF + 64)
+        make_z(sg_quarters[:, 1, :, :], HALF + 64, S)
+        quantise(HALF, S)
         second_product(0, HALF, S, 5)
         for m in range(1, 4):
             second_product(m, 0, S, (5 + m) % 8)

from contextlib import ExitStack

import concourse.mybir as mybir

K, T, S, N, G, H, U = 512, 1024, 256, 512, 2048, 512, 512
FLOPS = 2 * (2 * K * H * S + H * N * S)

F32 = mybir.dt.float32
BF16 = mybir.dt.bfloat16
I32 = mybir.dt.int32
U32 = mybir.dt.uint32
U16 = mybir.dt.uint16
U8 = mybir.dt.uint8
FP8X4 = mybir.dt.float8_e4m3fn_x4
FP4X4 = mybir.dt.float4_e2m1fn_x4
ACT = mybir.ActivationFunctionType
ALU = mybir.AluOpType

P = 128
PACK = 4
HALF = S // 2


def tile_picked_aqlehhpagmx_none_p_kernel(
    tc, x_words, x_scales, d_words, d_scales, sl, th, gn, w1_words, w1_scales, offs, ka, kb, n1, n2, n3, n4, n5, out
):
    nc = tc.nc
    with ExitStack() as ctx:
        sb = ctx.enter_context(tc.tile_pool(name="sb", bufs=1))
        psum = ctx.enter_context(tc.psum_pool(name="psum", bufs=1))

        def load_list(src, name):
            tile = sb.tile([P, src.shape[1]], U16, name=name)
            nc.sync.dma_start(tile[:], src)
            return tile

        def load_scale_window(scales, name):
            cols = scales.shape[2]
            tile = sb.tile([P, cols], U8, name=name, tag=name, align_bytes=64)
            rows = scales[0].bitcast(I32)
            nc.scalar.dma_start(tile[:].bitcast(I32), rows.unsqueeze(1).to_broadcast([16, 8, cols // 4]))
            return tile

        def load_word_window(words, name):
            tile = sb.tile([P, words.shape[2]], U32, name=name, tag=name, align_bytes=64)
            nc.scalar.dma_start(tile[:].bitcast(I32), words[0].rearrange("p n t -> p (n t)").bitcast(I32))
            return tile

        offs_l = load_list(offs, "offs_l")
        x_sc_win = load_scale_window(x_scales, "x_sc_win")
        ka_l = load_list(ka, "ka_l")
        d_sc_win = load_scale_window(d_scales, "d_sc_win")
        kb_l = load_list(kb, "kb_l")
        d_w_win = load_word_window(d_words, "d_w_win")
        x_w_win = load_word_window(x_words, "x_w_win")
        n1_l = load_list(n1, "n1_l")
        n2_l = load_list(n2, "n2_l")
        n5_l = load_list(n5, "n5_l")
        n3_l = load_list(n3, "n3_l")
        n4_l = load_list(n4, "n4_l")

        def load_column(src, name):
            tile = sb.tile([P, PACK], F32, name=name)
            nc.gpsimd.dma_start(tile[:], src.rearrange("(p t) o -> p (t o)", t=PACK))
            return tile

        sl_t = load_column(sl, "sl_t")
        th_t = load_column(th, "th_t")
        gn_t = load_column(gn, "gn_t")
        sl_th = sb.tile([P, PACK], F32, name="sl_th")
        nc.gpsimd.tensor_tensor(sl_th[:], sl_t[:], th_t[:], ALU.mult)
        bias = sb.tile([P, PACK], F32, name="bias")
        nc.gpsimd.tensor_scalar(bias[:], sl_th[:], -1.0, 0.0, ALU.mult, ALU.add)

        planes = sb.tile([P, H + S], U8, name="planes", align_bytes=64)
        nc.vector.memset(planes[:].bitcast(I32), 0)

        def window(name, width):
            tile = sb.tile([P, width], F32, name=name, tag=name)
            nc.vector.memset(tile[:, S:width], 0.0)
            return tile

        h_t = [window(f"h{t}", 2 * S) for t in range(PACK)]
        st_t = [sb.tile([P, S], F32, name=f"st{t}") for t in range(PACK)]
        h2_t = [window(f"h2_{m}", S + 16) for m in range(4)]

        warm = sb.tile([P, 1], F32, name="warm")
        nc.scalar.activation(warm[:], h_t[0][:, S : S + 1], ACT.Sigmoid)

        sc_b = sb.tile([P, H], U8, name="sc_b", tag="sc_b", align_bytes=64)
        sc_ax = sb.tile([P, H + S], U8, name="sc_ax", tag="sc_ax", align_bytes=64)
        nc.vector.tensor_copy(sc_ax[:, H : H + S], x_sc_win[:].indirect(offs_l[:]))
        nc.vector.tensor_copy(sc_ax[:, 0:H], d_sc_win[:].indirect(ka_l[:]))
        for i in range(4):
            nc.sync.dma_start(planes[i:P:32, :].bitcast(I32), sc_ax[8 * i : P : 32, :].bitcast(I32))
        nc.vector.tensor_copy(sc_b[:], d_sc_win[:].indirect(kb_l[:]))
        for i in range(4):
            nc.scalar.dma_start(planes[4 + i : P : 32, 0:H].bitcast(I32), sc_b[8 * i : P : 32, :].bitcast(I32))

        words = sb.tile([P, 2 * H + S], U32, name="words", tag="d_sc_win", align_bytes=64)
        xq = words[:, 2 * H : 2 * H + S]

        nc.vector.tensor_copy(words[:, 0:H], d_w_win[:].indirect(ka_l[:]))
        nc.vector.tensor_copy(words[:, H : 2 * H], d_w_win[:].indirect(kb_l[:]))
        nc.vector.tensor_copy(xq, x_w_win[:].indirect(offs_l[:]))

        got_w = words[:, 0 : 2 * H].bitcast(I32).rearrange("p (l m t) -> p l m t", l=2, t=PACK)
        got_p = planes[:, 0:H].rearrange("p (m t) -> p m t", t=PACK)

        def deal_words(name, t0, t1):
            dst = sb.tile([P, 2, t1 - t0, P], U32, name=name, tag=name, align_bytes=64)
            nc.vector.tensor_copy(dst[:].bitcast(I32).rearrange("p l t m -> p l m t"), got_w[:, :, :, t0:t1])
            return [dst[:, :, k, :] for k in range(t1 - t0)]

        def deal_planes(name, t0, t1):
            dst = sb.tile([P, t1 - t0, P], U8, name=name, align_bytes=64)
            nc.vector.tensor_copy(dst[:].rearrange("p t m -> p m t"), got_p[:, :, t0:t1])
            return [dst[:, k, :] for k in range(t1 - t0)]

        d_w = deal_words("w_first", 0, 1)
        d_planes = deal_planes("planes_first", 0, 1)
        d_w = d_w + deal_words("sc_b", 1, PACK)
        d_planes = d_planes + deal_planes("planes_rest", 1, PACK)

        w1_w = sb.tile([P, 2 * N], U8, name="w1_w", tag="x_w_win", align_bytes=64)
        w1_sc = sb.tile([P, N], U8, name="w1_sc", tag="d_w_win", align_bytes=64)
        nc.gpsimd.memset(w1_sc[:].bitcast(I32), 0)
        nc.sync.dma_start(w1_w[:].bitcast(I32), w1_words[0].bitcast(I32))
        for q in range(4):
            nc.sync.dma_start(w1_sc[32 * q : 32 * q + 4, :].bitcast(I32), w1_scales[0, 4 * q : 4 * q + 4, :].bitcast(I32))

        for t in range(PACK):
            acc = psum.tile([P, S], F32, name=f"acc_h{t}", tag=f"bank{t}")
            nc.tensor.matmul_mx(acc[:], lhsT=d_w[t][:, 0, :].bitcast(FP8X4), lhsT_scale=d_planes[t],
                                rhs=xq.bitcast(FP8X4), rhs_scale=planes[:, H : H + S], start=True, stop=False)
            nc.tensor.matmul_mx(acc[:], lhsT=d_w[t][:, 1, :].bitcast(FP8X4), lhsT_scale=d_planes[t][4:P, :],
                                rhs=xq.bitcast(FP8X4), rhs_scale=planes[:, H : H + S], start=False, stop=True)
            if t == 0:
                nc.scalar.activation(h_t[t][:, 0:S], acc[:], ACT.Copy, scale=0.0625)
            else:
                nc.vector.tensor_scalar(h_t[t][:, 0:S], acc[:], 0.0625, None, ALU.mult)

        for t in range(PACK):
            g1 = sb.tile([P, S], F32, name=f"g1_{t}", tag=f"g1_{t}")
            nc.scalar.activation(g1[:], h_t[t][:].indirect(n1_l[:]), ACT.Copy)
            nc.vector.tensor_tensor(st_t[t][:, 0:S], h_t[t][:, 0:S], g1[:], ALU.max)
        u = sb.tile([P, PACK, S], F32, name="u", tag="h3")
        for t in range(PACK):
            nc.vector.tensor_scalar(u[:, t, :], st_t[t][:], gn_t[:, t : t + 1], None, ALU.mult)

        zi = sb.tile([P, S, PACK], BF16, name="zi", align_bytes=64)
        z_codes = sb.tile([P, S], U32, name="z_codes", align_bytes=64)
        z_sc = sb.tile([P, S], U8, name="z_sc", align_bytes=64)

        def make_z(sg, lo, hi):
            for t in range(PACK):
                nc.scalar.activation(sg[:, t, :], st_t[t][:].indirect(n2_l[:, lo // 16 : hi // 16]), ACT.Sigmoid,
                                     bias=bias[:, t : t + 1], scale=sl_t[:, t : t + 1])
            nc.vector.tensor_tensor(
                zi[:, lo:hi, :].rearrange("p (c i) t -> p c t i", i=4),
                u[:, :, lo:hi].rearrange("p t (c i) -> p c t i", i=4),
                sg.rearrange("p t (c i) -> p c t i", i=4),
                ALU.mult,
            )

        def quantise(lo, hi):
            nc.vector.quantize_mx(z_codes[:, lo:hi].bitcast(FP8X4), z_sc[:, lo:hi], zi[:, lo:hi, :].rearrange("p c t -> p (c t)"))

        def second_product(m, lo, hi, bank):
            acc = psum.tile([P, hi - lo], F32, name=f"acc_o{m}_{lo}", tag=f"bank{bank}")
            nc.tensor.matmul_mx(acc[:], lhsT=w1_w[:, 2 * P * m : 2 * P * (m + 1)].bitcast(FP4X4),
                                lhsT_scale=w1_sc[:, P * m : P * (m + 1)],
                                rhs=z_codes[:, lo:hi].bitcast(FP8X4), rhs_scale=z_sc[:, lo:hi], start=True, stop=True)
            nc.vector.tensor_copy(h2_t[m][:, lo:hi], acc[:])

        sg_half = sb.tile([P, PACK, HALF], F32, name="sg_half", tag="g1_2")
        sg_quarters = sb.tile([P, 2, PACK, HALF // 2], F32, name="sg_quarters", tag="g1_3")
        make_z(sg_half[:], 0, HALF)
        quantise(0, HALF)
        second_product(0, 0, HALF, 4)
        make_z(sg_quarters[:, 0, :, :], HALF, HALF + 64)
        make_z(sg_quarters[:, 1, :, :], HALF + 64, S)
        quantise(HALF, S)
        second_product(0, HALF, S, 5)
        for m in range(1, 4):
            second_product(m, 0, S, (5 + m) % 8)

        g5_t, pages = [], []
        for m in range(4):
            g5 = sb.tile([P, S], F32, name=f"g5_{m}")
            nc.scalar.activation(g5[:], h2_t[m][:].indirect(n5_l[:]), ACT.Copy)
            g5_t.append(g5)
        for m in range(4):
            up = sb.tile([P, S], F32, name=f"up{m}", tag=f"put{m}")
            nc.vector.tensor_tensor(up[:], h2_t[m][:, 0:S], g5_t[m][:], ALU.max)
            page = sb.tile([P, U], F32, name=f"page{m}")
            nc.scalar.activation(page[:].indirect(n3_l[:]), up[:], ACT.Copy)
            pages.append(page)
        for m in range(4):
            dn = sb.tile([P, S], F32, name=f"dn{m}", tag=f"put{m}")
            nc.vector.tensor_tensor(dn[:], h2_t[m][:, 0:S], g5_t[m][:], ALU.min)
            nc.scalar.activation(pages[m][:].indirect(n4_l[:]), dn[:], ACT.Copy)
            nc.sync.dma_start(out[P * m : P * (m + 1), :], pages[m][:])
